import numpy as np
import ml_dtypes


def mxq(x, axis, fmt="e4m3"):
    dtype, down = {"e4m3": (ml_dtypes.float8_e4m3fn, 7), "e5m2": (ml_dtypes.float8_e5m2, 14)}[fmt]
    v = np.moveaxis(np.asarray(x, np.float32).astype(ml_dtypes.bfloat16).astype(np.float64), axis, -1)
    blocks = v.reshape(v.shape[:-1] + (-1, 32))
    amax = np.abs(blocks).max(-1, keepdims=True)
    byte = np.maximum(np.where(amax > 0, np.frexp(amax)[1] - 1 + 127, 0) - down, 1)
    scale = np.exp2(byte - 127.0)
    codes = (blocks / scale).astype(np.float32).astype(dtype).astype(np.float64)
    return np.moveaxis((codes * scale).reshape(v.shape), -1, axis)


WIDE = False


def mx_kscale(k):
    if not WIDE:
        return np.ones(k)
    levels = np.array([10, -10, 5, -5, 0])
    if k % 512:
        return np.exp2(np.random.permutation(np.resize(levels, k // 32))).repeat(32)
    a = np.empty((k // 512, 16))
    for p in range(k // 512):
        a[p, :8] = np.random.permutation(np.resize(levels, 8))
        for g in range(8):
            far = levels[np.abs(levels - a[p, g]) >= 10]
            a[p, g + 8] = far[np.random.randint(len(far))]
    return np.exp2(a.ravel()).repeat(32)


def f64(x):
    return np.asarray(x).astype(np.float64)


def striped(idx):
    return np.tile(idx.reshape(-1, 16).T, (8, 1)).astype(np.uint16)


def unstriped(offs):
    return offs[:16].T.reshape(-1).astype(np.int64)


def striped8(idx):
    return np.concatenate([x.reshape(-1, 16).T for x in idx]).astype(np.uint16)


def runs(offs, k):
    lists = np.stack([offs[16 * r : 16 * r + 16].T.reshape(-1) for r in range(8)]).astype(np.int64)
    return lists[np.arange(k) % 512 // 64]


def pack_weight(w):
    k, n = w.shape
    w = f64(np.asarray(w, np.float32).astype(ml_dtypes.bfloat16)).reshape(k // 32, 32, n)
    amax = np.abs(w).max(1)
    byte = np.clip(np.where(amax > 0, np.frexp(amax)[1] - 1 + 127 - 7, 1), 1, 254)
    scaled = (w * np.exp2(127.0 - byte)[:, None, :]).reshape(k, n).astype(np.float32)
    words = np.ascontiguousarray(scaled.reshape(k // 512, 128, 4, n).transpose(0, 1, 3, 2)).astype(ml_dtypes.float8_e4m3fn).view(np.uint8)
    return words, np.ascontiguousarray(byte.astype(np.uint8).reshape(k // 512, 16, n))


def unpack_weight(words, scales):
    g, p, n, _ = words.shape
    vals = np.ascontiguousarray(words).view(ml_dtypes.float8_e4m3fn).astype(np.float64) * np.repeat(np.exp2(scales.astype(np.float64) - 127.0), 8, axis=1)[..., None]
    return vals.transpose(0, 1, 3, 2).reshape(g * 512, n)


def sigmoid(v):
    return 1.0 / (1.0 + np.exp(-np.maximum(v, -700.0)))

def planes(y):
    n, m = y.shape
    v = y.astype(np.float32).astype(ml_dtypes.bfloat16).astype(np.float64).reshape(n // 32, 32, m)
    top = np.abs(v).max(1)
    byte = np.clip(np.where(top > 0, np.frexp(top)[1] - 1 + 127 - 7, 1), 1, 254)
    codes = (v * np.exp2(127.0 - byte)[:, None, :]).reshape(n, m).astype(np.float32).astype(ml_dtypes.float8_e4m3fn).view(np.uint8)
    words = codes.reshape(n // 512, 128, 4, m).transpose(0, 1, 3, 2)
    return np.ascontiguousarray(words), np.ascontiguousarray(byte.astype(np.uint8).reshape(n // 512, 16, m))


K, T, S, V, H, W = 512, 2048, 512, 512, 512, 256


def setup_inputs():
    n = np.random.standard_normal
    s = mx_kscale(K)[:, None]
    u = mx_kscale(S)
    packed_xT = pack_weight(n((K, T)) * s)
    packed_w1 = pack_weight(n((K, H)) / np.sqrt(K) / s)
    packed_w2 = pack_weight(n((K, H)) / np.sqrt(K) / s)
    packed_w3 = pack_weight(n((K, H)) / np.sqrt(K) / s)
    perm = np.stack([np.random.permutation(V) for _ in range(8)])
    return {
        "x_words": packed_xT[0],
        "x_scales": packed_xT[1],
        "w1_words": packed_w1[0],
        "w1_scales": packed_w1[1],
        "w2_words": packed_w2[0],
        "w2_scales": packed_w2[1],
        "w3_words": packed_w3[0],
        "w3_scales": packed_w3[1],
        "ga": (np.random.uniform(0.5, 1.5, (H, 1)) * u[:, None]).astype(np.float32),
        "gb": (np.random.uniform(0.5, 1.5, (H, 1)) / u[:, None]).astype(np.float32),
        "offs": striped(np.random.permutation(T)[:S]),
        "two": striped(np.random.permutation(T)[:S]),
        "n1": striped8(np.stack([np.random.permutation(S) for _ in range(8)])),
        "n2": striped8(np.stack([np.random.permutation(S) for _ in range(8)])),
        "three": striped(np.random.permutation(T)[:V]),
        "n3": striped8(np.stack([np.random.permutation(V) for _ in range(8)])),
        "n4": striped8(np.stack([np.random.permutation(V) for _ in range(8)])),
        "n5": striped8(perm[:, :W]),
        "n6": striped8(perm[:, W:]),
    }


def reference(x_words, x_scales, w1_words, w1_scales, w2_words, w2_scales, w3_words, w3_scales, ga, gb, offs, two, n1, n2, three, n3, n4, n5, n6):
    xq = unpack_weight(x_words, x_scales)[:, unstriped(offs)]
    y = unpack_weight(w1_words, w1_scales).T @ xq
    x_two = unpack_weight(x_words, x_scales)[:, unstriped(two)]
    d = unpack_weight(w2_words, w2_scales).T @ x_two
    z = f64(ga) * (y * (np.tanh(d[np.arange(H)[:, None], runs(n1, H)] - (d[np.arange(H)[:, None], runs(n2, H)]))))
    x_three = unpack_weight(x_words, x_scales)[:, unstriped(three)]
    b = unpack_weight(w3_words, w3_scales).T @ x_three
    z2 = f64(gb) * (b * (sigmoid(b[np.arange(H)[:, None], runs(n3, H)] - (b[np.arange(H)[:, None], runs(n4, H)]))))
    s = 0.0625 * ((mxq(z, 0, "e4m3").T @ mxq(z2, 0, "e4m3")))
    pa = s[np.arange(S)[:, None], runs(n5, S)]
    pb = s[np.arange(S)[:, None], runs(n6, S)]
    rb = pa * pb
    ra = pa + pb
    ds = np.zeros((S, V))
    ds[np.arange(S)[:, None], runs(n5, S)] = ra
    out = ds.copy()
    out[np.arange(S)[:, None], runs(n6, S)] = rb
    return (out,) + planes(out)

@@ -1,0 +1,247 @@
+from contextlib import ExitStack
+
+import concourse.mybir as mybir
+
+F32 = mybir.dt.float32
+BF16 = mybir.dt.bfloat16
+I32 = mybir.dt.int32
+U32 = mybir.dt.uint32
+U16 = mybir.dt.uint16
+U8 = mybir.dt.uint8
+FP8X4 = mybir.dt.float8_e4m3fn_x4
+ACT = mybir.ActivationFunctionType
+ALU = mybir.AluOpType
+
+P = 128
+PACK = 4
+T = 2048
+N = 512
+HALF = 256
+FLOPS = 4 * 2 * 512 * 512 * 512
+
+
+def tile_picked_twkjointbcmpbond_none_po_kernel(
+    tc, x_words, x_scales, w1_words, w1_scales, w2_words, w2_scales, w3_words, w3_scales,
+    ga, gb, offs, two, n1, n2, three, n3, n4, n5, n6, out_0, out_1, out_2,
+):
+    nc = tc.nc
+    with ExitStack() as ctx:
+        lists = ctx.enter_context(tc.tile_pool(name="lists", bufs=1))
+        sb = ctx.enter_context(tc.tile_pool(name="sb", bufs=1))
+        psum = ctx.enter_context(tc.psum_pool(name="psum", bufs=8))
+
+        def load_list(src, name):
+            tile = lists.tile(list(src.shape), U16, name=name)
+            nc.sync.dma_start(tile[:], src)
+            return tile
+
+        def load_scale_rows(queue, tile, src):
+            for quad in range(4):
+                queue.dma_start(tile[32 * quad : 32 * quad + 4, :], src[0, 4 * quad : 4 * quad + 4, :].bitcast(I32))
+
+        def load_words(src, cols, name):
+            tile = sb.tile([P, cols], I32, name=name, tag=name, align_bytes=64)
+            nc.sync.dma_start(tile[:], src[0].rearrange("p n t -> p (n t)").bitcast(I32))
+            return tile
+
+        def cleared(engine, cols, name):
+            tile = sb.tile([P, cols], I32, name=name, tag=name, align_bytes=64)
+            engine.memset(tile[:], 0)
+            return tile
+
+        def load_gain(src, name):
+            tiles = []
+            for t in range(PACK):
+                tile = sb.tile([P, 1], F32, name=f"{name}{t}")
+                with nc.allow_non_contiguous_dma(reason="one gain to a partition"):
+                    nc.sync.dma_start(tile[:], src.rearrange("(q t e) o -> t q e o", t=PACK, e=8)[t])
+                tiles.append(tile)
+            return tiles
+
+        xs = cleared(nc.vector, T // 4, "xs")
+        w3s = cleared(nc.gpsimd, N // 4, "w3s")
+        w2s = cleared(nc.gpsimd, N // 4, "w2s")
+        w1s = cleared(nc.gpsimd, N // 4, "w1s")
+
+        l_three = load_list(three, "l_three")
+        l_two = load_list(two, "l_two")
+        l_offs = load_list(offs, "l_offs")
+        load_scale_rows(nc.sync, xs, x_scales)
+        xw = load_words(x_words, T, "xw")
+        w3w = load_words(w3_words, N, "w3w")
+        load_scale_rows(nc.sync, w3s, w3_scales)
+        l_n4 = load_list(n4, "l_n4")
+        l_n3 = load_list(n3, "l_n3")
+        w2w = load_words(w2_words, N, "w2w")
+        load_scale_rows(nc.sync, w2s, w2_scales)
+        w1w = load_words(w1_words, N, "w1w")
+        load_scale_rows(nc.sync, w1s, w1_scales)
+        l_n2 = load_list(n2, "l_n2")
+        l_n1 = load_list(n1, "l_n1")
+        gb_t = load_gain(gb, "gb_t")
+        ga_t = load_gain(ga, "ga_t")
+        l_n5 = load_list(n5, "l_n5")
+        l_n6 = load_list(n6, "l_n6")
+
+        def pick_scales(lst, name):
+            tile = sb.tile([P, N], U8, name=name, align_bytes=64)
+            nc.vector.tensor_copy(tile[:], xs[:].bitcast(U8).indirect(lst[:]))
+            return tile
+
+        def pick_words(lst, name, tag):
+            tile = sb.tile([P, N], U32, name=name, tag=tag, align_bytes=64)
+            nc.vector.tensor_copy(tile[:], xw[:].bitcast(U32).indirect(lst[:]))
+            return tile
+
+        def deal(src, run, name):
+            tile = sb.tile(list(src.shape), I32, name=name, align_bytes=64)
+            nc.vector.tensor_copy(
+                tile[:].rearrange("p (t q e) -> p t q e", t=PACK, e=run),
+                src[:].rearrange("p (q t e) -> p t q e", t=PACK, e=run),
+            )
+            return tile
+
+        def project(ww, ws, xq, xq_s, name):
+            banks = []
+            for t in range(PACK):
+                bank = psum.tile([P, N], F32, name=name, tag="bank")
+                nc.tensor.matmul_mx(
+                    bank[:],
+                    lhsT=ww[:, P * t : P * (t + 1)].bitcast(FP8X4),
+                    lhsT_scale=ws[:, 32 * t : 32 * (t + 1)].bitcast(U8),
+                    rhs=xq[:].bitcast(FP8X4),
+                    rhs_scale=xq_s[:],
+                    start=True,
+                    stop=True,
+                )
+                banks.append(bank)
+            return banks
+
+        def windows(banks, name):
+            tiles = []
+            for t in range(PACK):
+                win = sb.tile([P, 2 * N], F32, name=f"{name}{t}")
+                nc.scalar.copy(win[:, :N], banks[t][:])
+                tiles.append(win)
+            return tiles
+
+        def differences(wins, plus, minus, name):
+            subs = [sb.tile([P, N], F32, name=f"{name}_m{t}") for t in range(PACK)]
+            diffs = [sb.tile([P, N], F32, name=f"{name}_d{t}") for t in range(PACK)]
+            nc.vector.tensor_copy(subs[0][:], wins[0][:].indirect(minus[:]))
+            for t in range(PACK):
+                if t + 1 < PACK:
+                    nc.vector.tensor_copy(subs[t + 1][:], wins[t + 1][:].indirect(minus[:]))
+                nc.vector.tensor_tensor(diffs[t][:], wins[t][:].indirect(plus[:]), subs[t][:], ALU.subtract)
+            return diffs
+
+        s_three = pick_scales(l_three, "s_three")
+        s_two = pick_scales(l_two, "s_two")
+        s_offs = pick_scales(l_offs, "s_offs")
+        x_three = pick_words(l_three, "x_three", "x_three")
+        w3d, w3sd = deal(w3w, 8, "w3d"), deal(w3s, 2, "w3sd")
+        b_banks = project(w3d, w3sd, x_three, s_three, "b")
+        b_wins = windows(b_banks, "b_win")
+        x_two = pick_words(l_two, "x_two", "w3w")
+        x_offs = pick_words(l_offs, "x_offs", "w3s")
+        w2d, w2sd = deal(w2w, 8, "w2d"), deal(w2s, 2, "w2sd")
+        w1d, w1sd = deal(w1w, 8, "w1d"), deal(w1s, 2, "w1sd")
+        d_banks = project(w2d, w2sd, x_two, s_two, "d")
+
+        bg = sb.tile([P, PACK, N], F32, name="bg")
+        for t in range(PACK):
+            nc.scalar.activation(bg[:, t, :], b_banks[t][:], ACT.Copy, scale=gb_t[t][:])
+        b_diffs = differences(b_wins, l_n3, l_n4, "b")
+        d_wins = windows(d_banks, "d_win")
+        gate = sb.tile([P, PACK, N], F32, name="gate")
+        for t in range(PACK):
+            nc.scalar.activation(gate[:, t, :], b_diffs[t][:], ACT.Sigmoid)
+
+        y_banks = project(w1d, w1sd, x_offs, s_offs, "y")
+        yg = sb.tile([P, PACK, PACK, P], F32, name="yg")
+        for t in range(PACK):
+            nc.scalar.activation(
+                yg[:, t, :, :], y_banks[t][:].rearrange("p (m u) -> p u m", u=PACK), ACT.Copy, scale=ga_t[t][:]
+            )
+
+        d_diffs = differences(d_wins, l_n1, l_n2, "d")
+        th = sb.tile([P, PACK, PACK, P], F32, name="th")
+        for t in range(PACK):
+            nc.scalar.activation(
+                th[:, t, :, :].rearrange("p u m -> p m u"), d_diffs[t][:].rearrange("p (m u) -> p m u", u=PACK), ACT.Tanh
+            )
+
+        z2b = sb.tile([P, N, PACK], BF16, name="z2b", align_bytes=64)
+        nc.vector.tensor_tensor(
+            z2b[:].rearrange("p (c i) t -> p c t i", i=4),
+            bg[:].rearrange("p t (c i) -> p c t i", i=4),
+            gate[:].rearrange("p t (c i) -> p c t i", i=4),
+            ALU.mult,
+        )
+        z2w = sb.tile([P, N], U32, name="z2w", align_bytes=64)
+        z2s = sb.tile([P, N], U8, name="z2s", align_bytes=64)
+
+        zb, s_wins = [], []
+
+        def multiply_z(u):
+            tile = sb.tile([P, P, PACK], BF16, name=f"zb{u}", align_bytes=64)
+            nc.vector.tensor_tensor(
+                tile[:].rearrange("p (c i) t -> p c t i", i=4),
+                yg[:, :, u, :].rearrange("p t (c i) -> p c t i", i=4),
+                th[:, :, u, :].rearrange("p t (c i) -> p c t i", i=4),
+                ALU.mult,
+            )
+            zb.append(tile)
+
+        def scores(u):
+            words = sb.tile([P, P], U32, name=f"zw{u}", align_bytes=64)
+            scales = sb.tile([P, P], U8, name=f"zs{u}", align_bytes=64)
+            nc.vector.quantize_mx(words[:].bitcast(FP8X4), scales[:], zb[u][:].rearrange("p m t -> p (m t)"))
+            bank = psum.tile([P, N], F32, name="s", tag="bank")
+            nc.tensor.matmul_mx(
+                bank[:], lhsT=words[:].bitcast(FP8X4), lhsT_scale=scales[:],
+                rhs=z2w[:].bitcast(FP8X4), rhs_scale=z2s[:], start=True, stop=True,
+            )
+            win = sb.tile([P, N], F32, name=f"s_win{u}")
+            nc.scalar.activation(win[:], bank[:], ACT.Copy, scale=0.0625)
+            s_wins.append(win)
+
+        multiply_z(0)
+        nc.vector.quantize_mx(z2w[:].bitcast(FP8X4), z2s[:], z2b[:].rearrange("p v t -> p (v t)"))
+        for u in range(PACK):
+            if u + 1 < PACK:
+                multiply_z(u + 1)
+            scores(u)
+
+        ob = sb.tile([P, N, PACK], BF16, name="ob", align_bytes=64)
+        rows = out_0.rearrange("(p u) v -> p u v", u=PACK)
+        pa = [sb.tile([P, HALF], F32, name=f"pa{u}") for u in range(PACK)]
+        pb = [sb.tile([P, HALF], F32, name=f"pb{u}") for u in range(PACK)]
+        res = [sb.tile([P, N], F32, name=f"res{u}") for u in range(PACK)]
+
+        def fetch(u):
+            nc.vector.tensor_copy(pa[u][:], s_wins[u][:].indirect(l_n5[:]))
+            nc.vector.tensor_copy(pb[u][:], s_wins[u][:].indirect(l_n6[:]))
+
+        def put_products(u):
+            nc.vector.tensor_tensor(res[u][:].indirect(l_n6[:]), pa[u][:], pb[u][:], ALU.mult)
+            nc.sync.dma_start(rows[:, u, :], res[u][:])
+            nc.scalar.copy(ob[:, :, u], res[u][:])
+
+        fetch(0)
+        for u in range(PACK):
+            if u + 1 < PACK:
+                fetch(u + 1)
+            if u > 0:
+                put_products(u - 1)
+            nc.vector.tensor_tensor(res[u][:].indirect(l_n5[:]), pa[u][:], pb[u][:], ALU.add)
+        put_products(PACK - 1)
+
+        ow = sb.tile([P, N], U32, name="ow", align_bytes=64)
+        os_ = sb.tile([P, N], U8, name="os_", align_bytes=64)
+        nc.vector.quantize_mx(ow[:].bitcast(FP8X4), os_[:], ob[:].rearrange("p v u -> p (v u)"))
+        nc.sync.dma_start(out_1[0].rearrange("p n t -> p (n t)").bitcast(I32), ow[:].bitcast(I32))
+        for quad in range(4):
+            nc.scalar.dma_start(
+                out_2[0, 4 * quad : 4 * quad + 4, :].bitcast(I32), os_[32 * quad : 32 * quad + 4, :].bitcast(I32)
+            )

@@ -17,6 +17,7 @@ PACK = 4
 T = 2048
 N = 512
 HALF = 256
+SHARE = 384
 FLOPS = 4 * 2 * 512 * 512 * 512
 
 
@@ -74,11 +75,11 @@ def tile_picked_twkjointbcmpbond_none_po_kernel(
         l_n3 = load_list(n3, "l_n3")
         w2w = load_words(w2_words, N, "w2w")
         load_scale_rows(nc.sync, w2s, w2_scales)
-        w1w = load_words(w1_words, N, "w1w")
-        load_scale_rows(nc.sync, w1s, w1_scales)
+        gb_t = load_gain(gb, "gb_t")
         l_n2 = load_list(n2, "l_n2")
         l_n1 = load_list(n1, "l_n1")
-        gb_t = load_gain(gb, "gb_t")
+        w1w = load_words(w1_words, N, "w1w")
+        load_scale_rows(nc.sync, w1s, w1_scales)
         ga_t = load_gain(ga, "ga_t")
         l_n5 = load_list(n5, "l_n5")
         l_n6 = load_list(n6, "l_n6")
@@ -120,20 +121,20 @@ def tile_picked_twkjointbcmpbond_none_po_kernel(
         def windows(banks, name):
             tiles = []
             for t in range(PACK):
-                win = sb.tile([P, 2 * N], F32, name=f"{name}{t}")
+                win = sb.tile([P, 2 * N], F32, name=f"{name}{t}", tag=f"{name}{t}")
                 nc.scalar.copy(win[:, :N], banks[t][:])
                 tiles.append(win)
             return tiles
 
-        def differences(wins, plus, minus, name):
-            subs = [sb.tile([P, N], F32, name=f"{name}_m{t}") for t in range(PACK)]
-            diffs = [sb.tile([P, N], F32, name=f"{name}_d{t}") for t in range(PACK)]
-            nc.vector.tensor_copy(subs[0][:], wins[0][:].indirect(minus[:]))
-            for t in range(PACK):
-                if t + 1 < PACK:
-                    nc.vector.tensor_copy(subs[t + 1][:], wins[t + 1][:].indirect(minus[:]))
-                nc.vector.tensor_tensor(diffs[t][:], wins[t][:].indirect(plus[:]), subs[t][:], ALU.subtract)
-            return diffs
+        def fetch_minus(wins, minus, name, t):
+            tile = sb.tile([P, N], F32, name=f"{name}_m{t}", tag=f"{name}_m{t}", align_bytes=64)
+            nc.vector.tensor_copy(tile[:], wins[t][:].indirect(minus[:]))
+            return tile
+
+        def difference(wins, plus, sub, name, t, tag):
+            tile = sb.tile([P, N], F32, name=f"{name}_d{t}", tag=tag)
+            nc.vector.tensor_tensor(tile[:], wins[t][:].indirect(plus[:]), sub, ALU.subtract)
+            return tile
 
         s_three = pick_scales(l_three, "s_three")
         s_two = pick_scales(l_two, "s_two")
@@ -142,8 +143,7 @@ def tile_picked_twkjointbcmpbond_none_po_kernel(
         w3d, w3sd = deal(w3w, 8, "w3d"), deal(w3s, 2, "w3sd")
         b_banks = project(w3d, w3sd, x_three, s_three, "b")
         b_wins = windows(b_banks, "b_win")
-        x_two = pick_words(l_two, "x_two", "w3w")
-        x_offs = pick_words(l_offs, "x_offs", "w3s")
+        x_two = pick_words(l_two, "x_two", "w3s")
         w2d, w2sd = deal(w2w, 8, "w2d"), deal(w2s, 2, "w2sd")
         w1d, w1sd = deal(w1w, 8, "w1d"), deal(w1s, 2, "w1sd")
         d_banks = project(w2d, w2sd, x_two, s_two, "d")
@@ -151,9 +151,15 @@ def tile_picked_twkjointbcmpbond_none_po_kernel(
         bg = sb.tile([P, PACK, N], F32, name="bg")
         for t in range(PACK):
             nc.scalar.activation(bg[:, t, :], b_banks[t][:], ACT.Copy, scale=gb_t[t][:])
-        b_diffs = differences(b_wins, l_n3, l_n4, "b")
+        b_subs = [fetch_minus(b_wins, l_n4, "b", 0)]
+        b_diffs = []
+        for t in range(PACK):
+            if t + 1 < PACK:
+                b_subs.append(fetch_minus(b_wins, l_n4, "b", t + 1))
+            b_diffs.append(difference(b_wins, l_n3, b_subs[t][:], "b", t, f"b_d{t}"))
+        x_offs = pick_words(l_offs, "x_offs", "b_m3")
         d_wins = windows(d_banks, "d_win")
-        gate = sb.tile([P, PACK, N], F32, name="gate")
+        gate = sb.tile([P, PACK, N], F32, name="gate", tag="gate")
         for t in range(PACK):
             nc.scalar.activation(gate[:, t, :], b_diffs[t][:], ACT.Sigmoid)
 
@@ -164,24 +170,34 @@ def tile_picked_twkjointbcmpbond_none_po_kernel(
                 yg[:, t, :, :], y_banks[t][:].rearrange("p (m u) -> p u m", u=PACK), ACT.Copy, scale=ga_t[t][:]
             )
 
-        d_diffs = differences(d_wins, l_n1, l_n2, "d")
+        z2b = sb.tile([P, N, PACK], BF16, name="z2b", align_bytes=64)
+
+        def multiply_z2(engine, cols):
+            engine.tensor_tensor(
+                z2b[:, cols, :].rearrange("p (c i) t -> p c t i", i=4),
+                bg[:, :, cols].rearrange("p t (c i) -> p c t i", i=4),
+                gate[:, :, cols].rearrange("p t (c i) -> p c t i", i=4),
+                ALU.mult,
+            )
+
+        multiply_z2(nc.gpsimd, slice(0, SHARE))
+        d_subs = sb.tile([P, PACK, N], F32, name="d_subs", tag="b_win3")
+        for t in range(PACK):
+            nc.vector.tensor_copy(d_subs[:, t, :], d_wins[t][:].indirect(l_n2[:]))
+        multiply_z2(nc.vector, slice(SHARE, N))
+        d_diffs = sb.tile([P, PACK, N], F32, name="d_diffs", tag="gate")
+        for t in range(PACK):
+            nc.vector.tensor_tensor(d_diffs[:, t, :], d_wins[t][:].indirect(l_n1[:]), d_subs[:, t, :], ALU.subtract)
         th = sb.tile([P, PACK, PACK, P], F32, name="th")
         for t in range(PACK):
             nc.scalar.activation(
-                th[:, t, :, :].rearrange("p u m -> p m u"), d_diffs[t][:].rearrange("p (m u) -> p m u", u=PACK), ACT.Tanh
+                th[:, t, :, :].rearrange("p u m -> p m u"), d_diffs[:, t, :].rearrange("p (m u) -> p m u", u=PACK), ACT.Tanh
             )
 
-        z2b = sb.tile([P, N, PACK], BF16, name="z2b", align_bytes=64)
-        nc.vector.tensor_tensor(
-            z2b[:].rearrange("p (c i) t -> p c t i", i=4),
-            bg[:].rearrange("p t (c i) -> p c t i", i=4),
-            gate[:].rearrange("p t (c i) -> p c t i", i=4),
-            ALU.mult,
-        )
         z2w = sb.tile([P, N], U32, name="z2w", align_bytes=64)
         z2s = sb.tile([P, N], U8, name="z2s", align_bytes=64)
 
-        zb, s_wins = [], []
+        zb, s_wins = {}, {}
 
         def multiply_z(u):
             tile = sb.tile([P, P, PACK], BF16, name=f"zb{u}", align_bytes=64)
@@ -191,7 +207,7 @@ def tile_picked_twkjointbcmpbond_none_po_kernel(
                 th[:, :, u, :].rearrange("p t (c i) -> p c t i", i=4),
                 ALU.mult,
             )
-            zb.append(tile)
+            zb[u] = tile
 
         def scores(u):
             words = sb.tile([P, P], U32, name=f"zw{u}", align_bytes=64)
@@ -204,14 +220,15 @@ def tile_picked_twkjointbcmpbond_none_po_kernel(
             )
             win = sb.tile([P, N], F32, name=f"s_win{u}")
             nc.scalar.activation(win[:], bank[:], ACT.Copy, scale=0.0625)
-            s_wins.append(win)
+            s_wins[u] = win
 
-        multiply_z(0)
         nc.vector.quantize_mx(z2w[:].bitcast(FP8X4), z2s[:], z2b[:].rearrange("p v t -> p (v t)"))
-        for u in range(PACK):
-            if u + 1 < PACK:
-                multiply_z(u + 1)
-            scores(u)
+        order = (2, 0, 1, 3)
+        multiply_z(order[0])
+        for step in range(PACK):
+            if step + 1 < PACK:
+                multiply_z(order[step + 1])
+            scores(order[step])
 
         ob = sb.tile([P, N, PACK], BF16, name="ob", align_bytes=64)
         rows = out_0.rearrange("(p u) v -> p u v", u=PACK)
@@ -226,22 +243,40 @@ def tile_picked_twkjointbcmpbond_none_po_kernel(
         def put_products(u):
             nc.vector.tensor_tensor(res[u][:].indirect(l_n6[:]), pa[u][:], pb[u][:], ALU.mult)
             nc.sync.dma_start(rows[:, u, :], res[u][:])
+
+        def put_sums(u):
+            nc.vector.tensor_tensor(res[u][:].indirect(l_n5[:]), pa[u][:], pb[u][:], ALU.add)
+
+        def round_rows(u):
             nc.scalar.copy(ob[:, :, u], res[u][:])
 
+        fetch(2)
         fetch(0)
-        for u in range(PACK):
-            if u + 1 < PACK:
-                fetch(u + 1)
-            if u > 0:
-                put_products(u - 1)
-            nc.vector.tensor_tensor(res[u][:].indirect(l_n5[:]), pa[u][:], pb[u][:], ALU.add)
-        put_products(PACK - 1)
+        put_sums(2)
+        fetch(1)
+        put_products(2)
+        nc.scalar.copy(ob[:, :, 2:4], res[2][:].unsqueeze(2).to_broadcast([P, N, 2]))
+        put_sums(0)
+        fetch(3)
+        put_products(0)
+        round_rows(0)
+        put_sums(1)
+        put_sums(3)
+        put_products(1)
+        round_rows(1)
+        put_products(3)
 
         ow = sb.tile([P, N], U32, name="ow", align_bytes=64)
         os_ = sb.tile([P, N], U8, name="os_", align_bytes=64)
-        nc.vector.quantize_mx(ow[:].bitcast(FP8X4), os_[:], ob[:].rearrange("p v u -> p (v u)"))
-        nc.sync.dma_start(out_1[0].rearrange("p n t -> p (n t)").bitcast(I32), ow[:].bitcast(I32))
+        halves = [slice(0, HALF), slice(HALF, N)]
+        for cols in halves:
+            nc.vector.tensor_copy(ob[:, cols, 3], res[3][:, cols])
+        out_words = out_1[0].rearrange("p n t -> p (n t)").bitcast(I32)
+        for cols in halves:
+            nc.vector.quantize_mx(ow[:, cols].bitcast(FP8X4), os_[:, cols], ob[:, cols, :].rearrange("p v u -> p (v u)"))
+            nc.sync.dma_start(out_words[:, cols], ow[:, cols].bitcast(I32))
         for quad in range(4):
-            nc.scalar.dma_start(
+            queue = nc.scalar if quad < 3 else nc.sync
+            queue.dma_start(
                 out_2[0, 4 * quad : 4 * quad + 4, :].bitcast(I32), os_[32 * quad : 32 * quad + 4, :].bitcast(I32)
             )

@@ -17,7 +17,6 @@ PACK = 4
 T = 2048
 N = 512
 HALF = 256
-SHARE = 384
 FLOPS = 4 * 2 * 512 * 512 * 512
 
 
@@ -75,11 +74,11 @@ def tile_picked_twkjointbcmpbond_none_po_kernel(
         l_n3 = load_list(n3, "l_n3")
         w2w = load_words(w2_words, N, "w2w")
         load_scale_rows(nc.sync, w2s, w2_scales)
+        w1w = load_words(w1_words, N, "w1w")
+        load_scale_rows(nc.sync, w1s, w1_scales)
         gb_t = load_gain(gb, "gb_t")
         l_n2 = load_list(n2, "l_n2")
         l_n1 = load_list(n1, "l_n1")
-        w1w = load_words(w1_words, N, "w1w")
-        load_scale_rows(nc.sync, w1s, w1_scales)
         ga_t = load_gain(ga, "ga_t")
         l_n5 = load_list(n5, "l_n5")
         l_n6 = load_list(n6, "l_n6")
@@ -94,9 +93,9 @@ def tile_picked_twkjointbcmpbond_none_po_kernel(
             nc.vector.tensor_copy(tile[:], xw[:].bitcast(U32).indirect(lst[:]))
             return tile
 
-        def deal(src, run, name):
+        def deal(engine, src, run, name):
             tile = sb.tile(list(src.shape), I32, name=name, align_bytes=64)
-            nc.vector.tensor_copy(
+            engine.tensor_copy(
                 tile[:].rearrange("p (t q e) -> p t q e", t=PACK, e=run),
                 src[:].rearrange("p (q t e) -> p t q e", t=PACK, e=run),
             )
@@ -131,37 +130,30 @@ def tile_picked_twkjointbcmpbond_none_po_kernel(
             nc.vector.tensor_copy(tile[:], wins[t][:].indirect(minus[:]))
             return tile
 
-        def difference(wins, plus, sub, name, t, tag):
-            tile = sb.tile([P, N], F32, name=f"{name}_d{t}", tag=tag)
-            nc.vector.tensor_tensor(tile[:], wins[t][:].indirect(plus[:]), sub, ALU.subtract)
-            return tile
-
         s_three = pick_scales(l_three, "s_three")
         s_two = pick_scales(l_two, "s_two")
         s_offs = pick_scales(l_offs, "s_offs")
         x_three = pick_words(l_three, "x_three", "x_three")
-        w3d, w3sd = deal(w3w, 8, "w3d"), deal(w3s, 2, "w3sd")
+        w3d, w3sd = deal(nc.vector, w3w, 8, "w3d"), deal(nc.vector, w3s, 2, "w3sd")
         b_banks = project(w3d, w3sd, x_three, s_three, "b")
         b_wins = windows(b_banks, "b_win")
         x_two = pick_words(l_two, "x_two", "w3s")
-        w2d, w2sd = deal(w2w, 8, "w2d"), deal(w2s, 2, "w2sd")
-        w1d, w1sd = deal(w1w, 8, "w1d"), deal(w1s, 2, "w1sd")
+        w2d, w2sd = deal(nc.gpsimd, w2w, 8, "w2d"), deal(nc.gpsimd, w2s, 2, "w2sd")
+        w1d, w1sd = deal(nc.gpsimd, w1w, 8, "w1d"), deal(nc.gpsimd, w1s, 2, "w1sd")
         d_banks = project(w2d, w2sd, x_two, s_two, "d")
 
         bg = sb.tile([P, PACK, N], F32, name="bg")
         for t in range(PACK):
             nc.scalar.activation(bg[:, t, :], b_banks[t][:], ACT.Copy, scale=gb_t[t][:])
-        b_subs = [fetch_minus(b_wins, l_n4, "b", 0)]
-        b_diffs = []
+        b_subs = [fetch_minus(b_wins, l_n4, "b", t) for t in range(PACK)]
+        b_diffs = sb.tile([P, PACK, N], F32, name="b_diffs")
         for t in range(PACK):
-            if t + 1 < PACK:
-                b_subs.append(fetch_minus(b_wins, l_n4, "b", t + 1))
-            b_diffs.append(difference(b_wins, l_n3, b_subs[t][:], "b", t, f"b_d{t}"))
+            nc.vector.tensor_tensor(b_diffs[:, t, :], b_wins[t][:].indirect(l_n3[:]), b_subs[t][:], ALU.subtract)
         x_offs = pick_words(l_offs, "x_offs", "b_m3")
         d_wins = windows(d_banks, "d_win")
         gate = sb.tile([P, PACK, N], F32, name="gate", tag="gate")
         for t in range(PACK):
-            nc.scalar.activation(gate[:, t, :], b_diffs[t][:], ACT.Sigmoid)
+            nc.scalar.activation(gate[:, t, :], b_diffs[:, t, :], ACT.Sigmoid)
 
         y_banks = project(w1d, w1sd, x_offs, s_offs, "y")
         yg = sb.tile([P, PACK, PACK, P], F32, name="yg")
@@ -170,21 +162,14 @@ def tile_picked_twkjointbcmpbond_none_po_kernel(
                 yg[:, t, :, :], y_banks[t][:].rearrange("p (m u) -> p u m", u=PACK), ACT.Copy, scale=ga_t[t][:]
             )
 
+        z2r = sb.tile([P, PACK, N], BF16, name="z2r")
+        for planes in (slice(0, PACK - 1), slice(PACK - 1, PACK)):
+            nc.gpsimd.tensor_tensor(z2r[:, planes, :], bg[:, planes, :], gate[:, planes, :], ALU.mult)
         z2b = sb.tile([P, N, PACK], BF16, name="z2b", align_bytes=64)
-
-        def multiply_z2(engine, cols):
-            engine.tensor_tensor(
-                z2b[:, cols, :].rearrange("p (c i) t -> p c t i", i=4),
-                bg[:, :, cols].rearrange("p t (c i) -> p c t i", i=4),
-                gate[:, :, cols].rearrange("p t (c i) -> p c t i", i=4),
-                ALU.mult,
-            )
-
-        multiply_z2(nc.gpsimd, slice(0, SHARE))
+        nc.scalar.copy(z2b[:].rearrange("p (c i) t -> p c t i", i=4), z2r[:].rearrange("p t (c i) -> p c t i", i=4))
         d_subs = sb.tile([P, PACK, N], F32, name="d_subs", tag="b_win3")
         for t in range(PACK):
             nc.vector.tensor_copy(d_subs[:, t, :], d_wins[t][:].indirect(l_n2[:]))
-        multiply_z2(nc.vector, slice(SHARE, N))
         d_diffs = sb.tile([P, PACK, N], F32, name="d_diffs", tag="gate")
         for t in range(PACK):
             nc.vector.tensor_tensor(d_diffs[:, t, :], d_wins[t][:].indirect(l_n1[:]), d_subs[:, t, :], ALU.subtract)

@@ -52,7 +52,7 @@ def tile_picked_twkjointbcmpbond_none_po_kernel(
         def load_gain(src, name):
             tiles = []
             for t in range(PACK):
-                tile = sb.tile([P, 1], F32, name=f"{name}{t}")
+                tile = sb.tile([P, 1], F32, name=f"{name}{t}", tag=f"{name}{t}")
                 with nc.allow_non_contiguous_dma(reason="one gain to a partition"):
                     nc.sync.dma_start(tile[:], src.rearrange("(q t e) o -> t q e o", t=PACK, e=8)[t])
                 tiles.append(tile)
@@ -88,10 +88,8 @@ def tile_picked_twkjointbcmpbond_none_po_kernel(
             nc.vector.tensor_copy(tile[:], xs[:].bitcast(U8).indirect(lst[:]))
             return tile
 
-        def pick_words(lst, name, tag):
-            tile = sb.tile([P, N], U32, name=name, tag=tag, align_bytes=64)
-            nc.vector.tensor_copy(tile[:], xw[:].bitcast(U32).indirect(lst[:]))
-            return tile
+        def pick_words(dst, lst):
+            nc.vector.tensor_copy(dst, xw[:].bitcast(U32).indirect(lst[:]))
 
         def deal(engine, src, run, name):
             tile = sb.tile(list(src.shape), I32, name=name, align_bytes=64)
@@ -109,7 +107,7 @@ def tile_picked_twkjointbcmpbond_none_po_kernel(
                     bank[:],
                     lhsT=ww[:, P * t : P * (t + 1)].bitcast(FP8X4),
                     lhsT_scale=ws[:, 32 * t : 32 * (t + 1)].bitcast(U8),
-                    rhs=xq[:].bitcast(FP8X4),
+                    rhs=xq.bitcast(FP8X4),
                     rhs_scale=xq_s[:],
                     start=True,
                     stop=True,
@@ -133,11 +131,16 @@ def tile_picked_twkjointbcmpbond_none_po_kernel(
         s_three = pick_scales(l_three, "s_three")
         s_two = pick_scales(l_two, "s_two")
         s_offs = pick_scales(l_offs, "s_offs")
-        x_three = pick_words(l_three, "x_three", "x_three")
+        x_first = sb.tile([P, N], U32, name="x_first", align_bytes=64)
+        x_three = x_first[:]
+        pick_words(x_three, l_three)
         w3d, w3sd = deal(nc.vector, w3w, 8, "w3d"), deal(nc.vector, w3s, 2, "w3sd")
         b_banks = project(w3d, w3sd, x_three, s_three, "b")
         b_wins = windows(b_banks, "b_win")
-        x_two = pick_words(l_two, "x_two", "w3s")
+        x_late = sb.tile([P, 2, N], U32, name="x_late", tag="w3s", align_bytes=64)
+        x_two, x_offs = x_late[:, 0, :], x_late[:, 1, :]
+        pick_words(x_two, l_two)
+        pick_words(x_offs, l_offs)
         w2d, w2sd = deal(nc.gpsimd, w2w, 8, "w2d"), deal(nc.gpsimd, w2s, 2, "w2sd")
         w1d, w1sd = deal(nc.gpsimd, w1w, 8, "w1d"), deal(nc.gpsimd, w1s, 2, "w1sd")
         d_banks = project(w2d, w2sd, x_two, s_two, "d")
@@ -146,31 +149,31 @@ def tile_picked_twkjointbcmpbond_none_po_kernel(
         for t in range(PACK):
             nc.scalar.activation(bg[:, t, :], b_banks[t][:], ACT.Copy, scale=gb_t[t][:])
         b_subs = [fetch_minus(b_wins, l_n4, "b", t) for t in range(PACK)]
-        b_diffs = sb.tile([P, PACK, N], F32, name="b_diffs")
+        b_diffs = [sb.tile([P, N], F32, name=f"b_diff{t}", tag=f"b_diff{t}") for t in range(PACK)]
         for t in range(PACK):
-            nc.vector.tensor_tensor(b_diffs[:, t, :], b_wins[t][:].indirect(l_n3[:]), b_subs[t][:], ALU.subtract)
-        x_offs = pick_words(l_offs, "x_offs", "b_m3")
+            nc.vector.tensor_tensor(b_diffs[t][:], b_wins[t][:].indirect(l_n3[:]), b_subs[t][:], ALU.subtract)
         d_wins = windows(d_banks, "d_win")
-        gate = sb.tile([P, PACK, N], F32, name="gate", tag="gate")
+        gate = sb.tile([P, PACK - 1, N], F32, name="gate", tag="gb_t2")
+        gate_last = sb.tile([P, N], F32, name="gate_last", tag="gb_t3")
         for t in range(PACK):
-            nc.scalar.activation(gate[:, t, :], b_diffs[:, t, :], ACT.Sigmoid)
+            nc.scalar.activation(gate[:, t, :] if t < PACK - 1 else gate_last[:], b_diffs[t][:], ACT.Sigmoid)
 
         y_banks = project(w1d, w1sd, x_offs, s_offs, "y")
-        yg = sb.tile([P, PACK, PACK, P], F32, name="yg")
+        yg = sb.tile([P, PACK, PACK, P], F32, name="yg", tag="b_diff3")
         for t in range(PACK):
             nc.scalar.activation(
                 yg[:, t, :, :], y_banks[t][:].rearrange("p (m u) -> p u m", u=PACK), ACT.Copy, scale=ga_t[t][:]
             )
 
         z2r = sb.tile([P, PACK, N], BF16, name="z2r")
-        for planes in (slice(0, PACK - 1), slice(PACK - 1, PACK)):
-            nc.gpsimd.tensor_tensor(z2r[:, planes, :], bg[:, planes, :], gate[:, planes, :], ALU.mult)
-        z2b = sb.tile([P, N, PACK], BF16, name="z2b", align_bytes=64)
-        nc.scalar.copy(z2b[:].rearrange("p (c i) t -> p c t i", i=4), z2r[:].rearrange("p t (c i) -> p c t i", i=4))
+        nc.gpsimd.tensor_tensor(z2r[:, : PACK - 1, :], bg[:, : PACK - 1, :], gate[:], ALU.mult)
         d_subs = sb.tile([P, PACK, N], F32, name="d_subs", tag="b_win3")
         for t in range(PACK):
             nc.vector.tensor_copy(d_subs[:, t, :], d_wins[t][:].indirect(l_n2[:]))
-        d_diffs = sb.tile([P, PACK, N], F32, name="d_diffs", tag="gate")
+        nc.vector.tensor_tensor(z2r[:, PACK - 1, :], bg[:, PACK - 1, :], gate_last[:], ALU.mult)
+        z2b = sb.tile([P, N, PACK], BF16, name="z2b", align_bytes=64)
+        nc.scalar.copy(z2b[:].rearrange("p (c i) t -> p c t i", i=4), z2r[:].rearrange("p t (c i) -> p c t i", i=4))
+        d_diffs = sb.tile([P, PACK, N], F32, name="d_diffs", tag="gb_t2")
         for t in range(PACK):
             nc.vector.tensor_tensor(d_diffs[:, t, :], d_wins[t][:].indirect(l_n1[:]), d_subs[:, t, :], ALU.subtract)
         th = sb.tile([P, PACK, PACK, P], F32, name="th")

from contextlib import ExitStack

import concourse.mybir as mybir

F32 = mybir.dt.float32
BF16 = mybir.dt.bfloat16
I32 = mybir.dt.int32
U32 = mybir.dt.uint32
U16 = mybir.dt.uint16
U8 = mybir.dt.uint8
FP8X4 = mybir.dt.float8_e4m3fn_x4
ACT = mybir.ActivationFunctionType
ALU = mybir.AluOpType

P = 128
PACK = 4
T = 2048
N = 512
HALF = 256
FLOPS = 4 * 2 * 512 * 512 * 512


def tile_picked_twkjointbcmpbond_none_po_kernel(
    tc, x_words, x_scales, w1_words, w1_scales, w2_words, w2_scales, w3_words, w3_scales,
    ga, gb, offs, two, n1, n2, three, n3, n4, n5, n6, out_0, out_1, out_2,
):
    nc = tc.nc
    with ExitStack() as ctx:
        lists = ctx.enter_context(tc.tile_pool(name="lists", bufs=1))
        sb = ctx.enter_context(tc.tile_pool(name="sb", bufs=1))
        psum = ctx.enter_context(tc.psum_pool(name="psum", bufs=8))

        def load_list(src, name):
            tile = lists.tile(list(src.shape), U16, name=name)
            nc.sync.dma_start(tile[:], src)
            return tile

        def load_scale_rows(queue, tile, src):
            for quad in range(4):
                queue.dma_start(tile[32 * quad : 32 * quad + 4, :], src[0, 4 * quad : 4 * quad + 4, :].bitcast(I32))

        def load_words(src, cols, name):
            tile = sb.tile([P, cols], I32, name=name, tag=name, align_bytes=64)
            nc.sync.dma_start(tile[:], src[0].rearrange("p n t -> p (n t)").bitcast(I32))
            return tile

        def cleared(engine, cols, name):
            tile = sb.tile([P, cols], I32, name=name, tag=name, align_bytes=64)
            engine.memset(tile[:], 0)
            return tile

        def load_gain(src, name):
            tiles = []
            for t in range(PACK):
                tile = sb.tile([P, 1], F32, name=f"{name}{t}", tag=f"{name}{t}")
                with nc.allow_non_contiguous_dma(reason="one gain to a partition"):
                    nc.sync.dma_start(tile[:], src.rearrange("(q t e) o -> t q e o", t=PACK, e=8)[t])
                tiles.append(tile)
            return tiles

        xs = cleared(nc.vector, T // 4, "xs")
        w3s = cleared(nc.gpsimd, N // 4, "w3s")
        w2s = cleared(nc.gpsimd, N // 4, "w2s")
        w1s = cleared(nc.gpsimd, N // 4, "w1s")

        l_three = load_list(three, "l_three")
        l_two = load_list(two, "l_two")
        l_offs = load_list(offs, "l_offs")
        load_scale_rows(nc.sync, xs, x_scales)
        xw = load_words(x_words, T, "xw")
        w3w = load_words(w3_words, N, "w3w")
        load_scale_rows(nc.sync, w3s, w3_scales)
        l_n4 = load_list(n4, "l_n4")
        l_n3 = load_list(n3, "l_n3")
        w2w = load_words(w2_words, N, "w2w")
        load_scale_rows(nc.sync, w2s, w2_scales)
        w1w = load_words(w1_words, N, "w1w")
        load_scale_rows(nc.sync, w1s, w1_scales)
        gb_t = load_gain(gb, "gb_t")
        l_n2 = load_list(n2, "l_n2")
        l_n1 = load_list(n1, "l_n1")
        ga_t = load_gain(ga, "ga_t")
        l_n5 = load_list(n5, "l_n5")
        l_n6 = load_list(n6, "l_n6")

        def pick_scales(lst, name):
            tile = sb.tile([P, N], U8, name=name, align_bytes=64)
            nc.vector.tensor_copy(tile[:], xs[:].bitcast(U8).indirect(lst[:]))
            return tile

        def pick_words(dst, lst):
            nc.vector.tensor_copy(dst, xw[:].bitcast(U32).indirect(lst[:]))

        def deal(engine, src, run, name):
            tile = sb.tile(list(src.shape), I32, name=name, align_bytes=64)
            engine.tensor_copy(
                tile[:].rearrange("p (t q e) -> p t q e", t=PACK, e=run),
                src[:].rearrange("p (q t e) -> p t q e", t=PACK, e=run),
            )
            return tile

        def project(ww, ws, xq, xq_s, name):
            banks = []
            for t in range(PACK):
                bank = psum.tile([P, N], F32, name=name, tag="bank")
                nc.tensor.matmul_mx(
                    bank[:],
                    lhsT=ww[:, P * t : P * (t + 1)].bitcast(FP8X4),
                    lhsT_scale=ws[:, 32 * t : 32 * (t + 1)].bitcast(U8),
                    rhs=xq.bitcast(FP8X4),
                    rhs_scale=xq_s[:],
                    start=True,
                    stop=True,
                )
                banks.append(bank)
            return banks

        def windows(banks, name):
            tiles = []
            for t in range(PACK):
                win = sb.tile([P, 2 * N], F32, name=f"{name}{t}", tag=f"{name}{t}")
                nc.scalar.copy(win[:, :N], banks[t][:])
                tiles.append(win)
            return tiles

        def fetch_minus(wins, minus, name, t):
            tile = sb.tile([P, N], F32, name=f"{name}_m{t}", tag=f"{name}_m{t}", align_bytes=64)
            nc.vector.tensor_copy(tile[:], wins[t][:].indirect(minus[:]))
            return tile

        s_three = pick_scales(l_three, "s_three")
        s_two = pick_scales(l_two, "s_two")
        s_offs = pick_scales(l_offs, "s_offs")
        x_first = sb.tile([P, N], U32, name="x_first", align_bytes=64)
        x_three = x_first[:]
        pick_words(x_three, l_three)
        w3d, w3sd = deal(nc.vector, w3w, 8, "w3d"), deal(nc.vector, w3s, 2, "w3sd")
        b_banks = project(w3d, w3sd, x_three, s_three, "b")
        b_wins = windows(b_banks, "b_win")
        x_late = sb.tile([P, 2, N], U32, name="x_late", tag="w3s", align_bytes=64)
        x_two, x_offs = x_late[:, 0, :], x_late[:, 1, :]
        pick_words(x_two, l_two)
        pick_words(x_offs, l_offs)
        w2d, w2sd = deal(nc.gpsimd, w2w, 8, "w2d"), deal(nc.gpsimd, w2s, 2, "w2sd")
        w1d, w1sd = deal(nc.gpsimd, w1w, 8, "w1d"), deal(nc.gpsimd, w1s, 2, "w1sd")
        d_banks = project(w2d, w2sd, x_two, s_two, "d")

        bg = sb.tile([P, PACK, N], F32, name="bg")
        for t in range(PACK):
            nc.scalar.activation(bg[:, t, :], b_banks[t][:], ACT.Copy, scale=gb_t[t][:])
        b_subs = [fetch_minus(b_wins, l_n4, "b", t) for t in range(PACK)]
        b_diffs = [sb.tile([P, N], F32, name=f"b_diff{t}", tag=f"b_diff{t}") for t in range(PACK)]
        for t in range(PACK):
            nc.vector.tensor_tensor(b_diffs[t][:], b_wins[t][:].indirect(l_n3[:]), b_subs[t][:], ALU.subtract)
        d_wins = windows(d_banks, "d_win")
        gate = sb.tile([P, PACK - 1, N], F32, name="gate", tag="gb_t2")
        gate_last = sb.tile([P, N], F32, name="gate_last", tag="gb_t3")
        for t in range(PACK):
            nc.scalar.activation(gate[:, t, :] if t < PACK - 1 else gate_last[:], b_diffs[t][:], ACT.Sigmoid)

        y_banks = project(w1d, w1sd, x_offs, s_offs, "y")
        yg = sb.tile([P, PACK, PACK, P], F32, name="yg", tag="b_diff3")
        for t in range(PACK):
            nc.scalar.activation(
                yg[:, t, :, :], y_banks[t][:].rearrange("p (m u) -> p u m", u=PACK), ACT.Copy, scale=ga_t[t][:]
            )

        z2r = sb.tile([P, PACK, N], BF16, name="z2r")
        nc.gpsimd.tensor_tensor(z2r[:, : PACK - 1, :], bg[:, : PACK - 1, :], gate[:], ALU.mult)
        d_subs = sb.tile([P, PACK, N], F32, name="d_subs", tag="b_win3")
        for t in range(PACK):
            nc.vector.tensor_copy(d_subs[:, t, :], d_wins[t][:].indirect(l_n2[:]))
        nc.vector.tensor_tensor(z2r[:, PACK - 1, :], bg[:, PACK - 1, :], gate_last[:], ALU.mult)
        z2b = sb.tile([P, N, PACK], BF16, name="z2b", align_bytes=64)
        nc.scalar.copy(z2b[:].rearrange("p (c i) t -> p c t i", i=4), z2r[:].rearrange("p t (c i) -> p c t i", i=4))
        d_diffs = sb.tile([P, PACK, N], F32, name="d_diffs", tag="gb_t2")
        for t in range(PACK):
            nc.vector.tensor_tensor(d_diffs[:, t, :], d_wins[t][:].indirect(l_n1[:]), d_subs[:, t, :], ALU.subtract)
        th = sb.tile([P, PACK, PACK, P], F32, name="th")
        for t in range(PACK):
            nc.scalar.activation(
                th[:, t, :, :].rearrange("p u m -> p m u"), d_diffs[:, t, :].rearrange("p (m u) -> p m u", u=PACK), ACT.Tanh
            )

        z2w = sb.tile([P, N], U32, name="z2w", align_bytes=64)
        z2s = sb.tile([P, N], U8, name="z2s", align_bytes=64)

        zb, s_wins = {}, {}

        def multiply_z(u):
            tile = sb.tile([P, P, PACK], BF16, name=f"zb{u}", align_bytes=64)
            nc.vector.tensor_tensor(
                tile[:].rearrange("p (c i) t -> p c t i", i=4),
                yg[:, :, u, :].rearrange("p t (c i) -> p c t i", i=4),
                th[:, :, u, :].rearrange("p t (c i) -> p c t i", i=4),
                ALU.mult,
            )
            zb[u] = tile

        def scores(u):
            words = sb.tile([P, P], U32, name=f"zw{u}", align_bytes=64)
            scales = sb.tile([P, P], U8, name=f"zs{u}", align_bytes=64)
            nc.vector.quantize_mx(words[:].bitcast(FP8X4), scales[:], zb[u][:].rearrange("p m t -> p (m t)"))
            bank = psum.tile([P, N], F32, name="s", tag="bank")
            nc.tensor.matmul_mx(
                bank[:], lhsT=words[:].bitcast(FP8X4), lhsT_scale=scales[:],
                rhs=z2w[:].bitcast(FP8X4), rhs_scale=z2s[:], start=True, stop=True,
            )
            win = sb.tile([P, N], F32, name=f"s_win{u}")
            nc.scalar.activation(win[:], bank[:], ACT.Copy, scale=0.0625)
            s_wins[u] = win

        nc.vector.quantize_mx(z2w[:].bitcast(FP8X4), z2s[:], z2b[:].rearrange("p v t -> p (v t)"))
        order = (2, 0, 1, 3)
        multiply_z(order[0])
        for step in range(PACK):
            if step + 1 < PACK:
                multiply_z(order[step + 1])
            scores(order[step])

        ob = sb.tile([P, N, PACK], BF16, name="ob", align_bytes=64)
        rows = out_0.rearrange("(p u) v -> p u v", u=PACK)
        pa = [sb.tile([P, HALF], F32, name=f"pa{u}") for u in range(PACK)]
        pb = [sb.tile([P, HALF], F32, name=f"pb{u}") for u in range(PACK)]
        res = [sb.tile([P, N], F32, name=f"res{u}") for u in range(PACK)]

        def fetch(u):
            nc.vector.tensor_copy(pa[u][:], s_wins[u][:].indirect(l_n5[:]))
            nc.vector.tensor_copy(pb[u][:], s_wins[u][:].indirect(l_n6[:]))

        def put_products(u):
            nc.vector.tensor_tensor(res[u][:].indirect(l_n6[:]), pa[u][:], pb[u][:], ALU.mult)
            nc.sync.dma_start(rows[:, u, :], res[u][:])

        def put_sums(u):
            nc.vector.tensor_tensor(res[u][:].indirect(l_n5[:]), pa[u][:], pb[u][:], ALU.add)

        def round_rows(u):
            nc.scalar.copy(ob[:, :, u], res[u][:])

        fetch(2)
        fetch(0)
        put_sums(2)
        fetch(1)
        put_products(2)
        nc.scalar.copy(ob[:, :, 2:4], res[2][:].unsqueeze(2).to_broadcast([P, N, 2]))
        put_sums(0)
        fetch(3)
        put_products(0)
        round_rows(0)
        put_sums(1)
        put_sums(3)
        put_products(1)
        round_rows(1)
        put_products(3)

        ow = sb.tile([P, N], U32, name="ow", align_bytes=64)
        os_ = sb.tile([P, N], U8, name="os_", align_bytes=64)
        halves = [slice(0, HALF), slice(HALF, N)]
        for cols in halves:
            nc.vector.tensor_copy(ob[:, cols, 3], res[3][:, cols])
        out_words = out_1[0].rearrange("p n t -> p (n t)").bitcast(I32)
        for cols in halves:
            nc.vector.quantize_mx(ow[:, cols].bitcast(FP8X4), os_[:, cols], ob[:, cols, :].rearrange("p v u -> p (v u)"))
            nc.sync.dma_start(out_words[:, cols], ow[:, cols].bitcast(I32))
        for quad in range(4):
            queue = nc.scalar if quad < 3 else nc.sync
            queue.dma_start(
                out_2[0, 4 * quad : 4 * quad + 4, :].bitcast(I32), os_[32 * quad : 32 * quad + 4, :].bitcast(I32)
            )
